import numpy as np
import ml_dtypes


def mxq(x, axis, fmt="e4m3"):
    dtype, down = {"e4m3": (ml_dtypes.float8_e4m3fn, 7), "e5m2": (ml_dtypes.float8_e5m2, 14)}[fmt]
    v = np.moveaxis(np.asarray(x, np.float32).astype(ml_dtypes.bfloat16).astype(np.float64), axis, -1)
    blocks = v.reshape(v.shape[:-1] + (-1, 32))
    amax = np.abs(blocks).max(-1, keepdims=True)
    byte = np.maximum(np.where(amax > 0, np.frexp(amax)[1] - 1 + 127, 0) - down, 1)
    scale = np.exp2(byte - 127.0)
    codes = (blocks / scale).astype(np.float32).astype(dtype).astype(np.float64)
    return np.moveaxis((codes * scale).reshape(v.shape), -1, axis)


WIDE = False


def mx_kscale(k):
    if not WIDE:
        return np.ones(k)
    levels = np.array([10, -10, 5, -5, 0])
    if k % 512:
        return np.exp2(np.random.permutation(np.resize(levels, k // 32))).repeat(32)
    a = np.empty((k // 512, 16))
    for p in range(k // 512):
        a[p, :8] = np.random.permutation(np.resize(levels, 8))
        for g in range(8):
            far = levels[np.abs(levels - a[p, g]) >= 10]
            a[p, g + 8] = far[np.random.randint(len(far))]
    return np.exp2(a.ravel()).repeat(32)


def f64(x):
    return np.asarray(x).astype(np.float64)


def striped(idx):
    return np.tile(idx.reshape(-1, 16).T, (8, 1)).astype(np.uint16)


def unstriped(offs):
    return offs[:16].T.reshape(-1).astype(np.int64)


E2M1 = np.array([0.0, 0.5, 1.0, 1.5, 2.0, 3.0, 4.0, 6.0, -0.0, -0.5, -1.0, -1.5, -2.0, -3.0, -4.0, -6.0])


def pack_weight(w, fmt):
    k, n = w.shape
    w = f64(np.asarray(w, np.float32).astype(ml_dtypes.bfloat16)).reshape(k // 32, 32, n)
    amax = np.abs(w).max(1)
    if fmt == "e4m3":
        byte = np.frexp(amax)[1] - 1 + 127 - 7
    else:
        mant, ex = np.frexp(amax / 6.0)
        byte = np.where(mant > 0.5, ex, ex - 1) + 127
    byte = np.clip(np.where(amax > 0, byte, 1), 1, 254)
    scaled = (w * np.exp2(127.0 - byte)[:, None, :]).reshape(k, n).astype(np.float32)
    by_word = np.ascontiguousarray(scaled.reshape(k // 512, 128, 4, n).transpose(0, 1, 3, 2))
    if fmt == "e4m3":
        words = by_word.astype(ml_dtypes.float8_e4m3fn).view(np.uint8)
    else:
        c = by_word.astype(ml_dtypes.float4_e2m1fn).view(np.uint8) & 0xF
        words = (c[..., 0::2] | (c[..., 1::2] << 4)).reshape(k // 512, 128, 2 * n)
    return np.ascontiguousarray(words), np.ascontiguousarray(byte.astype(np.uint8).reshape(k // 512, 16, n))


def unpack_weight(words, scales, fmt):
    g, _, n = scales.shape
    words = np.ascontiguousarray(words).reshape(g, 128, n, -1)
    if fmt == "e4m3":
        vals = words.view(ml_dtypes.float8_e4m3fn).astype(np.float64)
    else:
        nib = np.empty((g, 128, n, 4), np.uint8)
        nib[..., 0::2] = words & 0xF
        nib[..., 1::2] = words >> 4
        vals = E2M1[nib]
    vals = vals * np.repeat(np.exp2(scales.astype(np.float64) - 127.0), 8, axis=1)[..., None]
    return vals.transpose(0, 1, 3, 2).reshape(g * 512, n)


def gelu(v):
    return 0.5 * v * (1.0 + np.tanh(np.sqrt(2.0 / np.pi) * (v + 0.044715 * v**3)))


K, K2, T, T3, H, N, S, P = 1024, 512, 4096, 2048, 1024, 512, 1024, 512


def setup_inputs():
    n = np.random.standard_normal
    s = mx_kscale(K)[:, None]
    s2 = mx_kscale(K2)[:, None]
    u = mx_kscale(H)[:, None]
    d = {}
    d["tab_words"], d["tab_scales"] = pack_weight(n((K, T)) * s, "e4m3")
    d["tab2_words"], d["tab2_scales"] = pack_weight(n((K2, T3)) * s2, "e4m3")
    d["offs"] = striped(np.random.permutation(T)[:S])
    d["offs2"] = striped(np.random.permutation(T3)[:P])
    d["pos1"] = striped(np.random.permutation(S)[:P])
    d["w1"] = (0.8 * n((H, K)).T / K ** 0.5 / s * u.T).astype(np.float32)
    d["b1"] = (0.5 * n(H) * u[:, 0]).astype(np.float32)
    d["w2_words"], d["w2_scales"] = pack_weight(1.3 * n((K2, H)) / K2 ** 0.5 / s2, "e2m1")
    d["wgs"] = np.exp(0.3 * n((128, P))).astype(np.float32)
    d["w3"] = (n((H, N)) / H ** 0.5 / u).astype(np.float32)
    d["w4_words"], d["w4_scales"] = pack_weight(0.8 * n((H, N)) / H ** 0.5 / u, "e4m3")
    return d


def reference(tab_words, tab_scales, tab2_words, tab2_scales, offs, offs2, pos1,
              w1, b1, w2_words, w2_scales, wgs, w3, w4_words, w4_scales):
    v = unpack_weight(tab_words, tab_scales, "e4m3")[:, unstriped(offs)]
    v2 = unpack_weight(tab2_words, tab2_scales, "e4m3")[:, unstriped(offs2)]
    a = (mxq(f64(w1), 0, "e4m3").T @ v) + f64(b1)[:, None]
    b = np.exp(np.tanh(unpack_weight(w2_words, w2_scales, "e2m1").T @ v2))
    placed = np.zeros((H, S))
    placed[:, unstriped(pos1)] = np.tile(f64(wgs), (H // 128, 1)) * b
    zq = mxq(a * (1.0 + placed), 0, "e4m3")
    y = mxq(f64(w3), 0, "e4m3").T @ zq
    y4 = unpack_weight(w4_words, w4_scales, "e4m3").T @ zq
    return y / (1.0 + np.exp(-y)) + y4

@@ -1,0 +1,323 @@
+from contextlib import ExitStack
+
+import concourse.mybir as mybir
+
+K, K2, T, T3, H, N, S, R = 1024, 512, 4096, 2048, 1024, 512, 1024, 512
+FLOPS = 2 * (K * H * S + K2 * H * R + 2 * H * N * S)
+
+F32 = mybir.dt.float32
+BF16 = mybir.dt.bfloat16
+I32 = mybir.dt.int32
+U32 = mybir.dt.uint32
+U16 = mybir.dt.uint16
+U8 = mybir.dt.uint8
+FP8X4 = mybir.dt.float8_e4m3fn_x4
+FP4X4 = mybir.dt.float4_e2m1fn_x4
+ACT = mybir.ActivationFunctionType
+ALU = mybir.AluOpType
+
+P = 128
+PACK = 4
+KP = 512
+W = 512
+
+
+def tile_list_note_fitness_scores_kernel(
+    tc, tab_words, tab_scales, tab2_words, tab2_scales, offs, offs2, pos1,
+    w1, b1, w2_words, w2_scales, wgs, w3, w4_words, w4_scales, out,
+):
+    nc = tc.nc
+    with ExitStack() as ctx:
+        held = ctx.enter_context(tc.tile_pool(name="held", bufs=1))
+        ring = ctx.enter_context(tc.tile_pool(name="ring", bufs=1))
+        psum = ctx.enter_context(tc.psum_pool(name="psum", bufs=1))
+
+        def keep(shape, dtype, name):
+            return held.tile(shape, dtype, name=name, align_bytes=64)
+
+        def raw_tile(dtype, name):
+            return ring.tile([P, 2048], dtype, name=name, tag="raw", bufs=3, align_bytes=64)
+
+        def woven_tile(name):
+            return ring.tile([P, 2048], BF16, name=name, tag="woven", bufs=4, align_bytes=64)
+
+        def cols_tile(name):
+            return ring.tile([P, W], F32, name=name, tag="cols", bufs=16, align_bytes=64)
+
+        def slot(tag, shape, dtype, name):
+            if tag == "raw":
+                return ring.tile(shape, dtype, name=name, tag=tag, bufs=3, align_bytes=64)
+            return ring.tile(shape, dtype, name=name, tag=tag, bufs=1, align_bytes=64)
+
+        def load_scale_rows(plane, scales, zeroing, queues):
+            passes = scales.shape[0]
+            zeroing.memset(plane[:].bitcast(I32), 0)
+            for q in range(4):
+                queues[q].dma_start(
+                    out=plane[32 * q : 32 * q + 4 * passes, :].bitcast(I32),
+                    in_=scales[:, 4 * q : 4 * q + 4, :].bitcast(I32),
+                )
+
+        on_sync = [nc.sync] * 4
+
+        idx2 = held.tile([P, R // 16], U16, name="idx2")
+        nc.sync.dma_start(idx2[:], offs2)
+        w2_raw = slot("gains0", [P, 2 * H], U8, "w2_raw")
+        nc.sync.dma_start(out=w2_raw[:].bitcast(I32), in_=w2_words[0].bitcast(I32))
+        places = held.tile([P, R // 16], U16, name="places")
+        nc.sync.dma_start(places[:], pos1)
+        idx = held.tile([P, S // 16], U16, name="idx")
+        nc.sync.dma_start(idx[:], offs)
+        tab2 = raw_tile(U32, "tab2")
+        nc.sync.dma_start(out=tab2[:].bitcast(I32), in_=tab2_words[0].rearrange("p t i -> p (t i)").bitcast(I32))
+        tab2_plane = slot("tab_plane", [P, T3], U8, "tab2_plane")
+        load_scale_rows(tab2_plane, tab2_scales, nc.vector, on_sync)
+        w2_plane_raw = slot("raw", [P, H], U8, "w2_plane_raw")
+        load_scale_rows(w2_plane_raw, w2_scales, nc.vector, [nc.sync, nc.sync, nc.sync, nc.gpsimd])
+
+        wgs_rows = wgs.rearrange("(q t) j -> q t j", t=PACK)
+        gains = {}
+
+        def load_gains(u):
+            gains[u] = slot("gains%d" % u, [P, 2, R], F32, "gains%d" % u)
+            for g in range(4):
+                nc.sync.dma_start(out=gains[u][32 * g : 32 * g + 32, :, :], in_=wgs_rows[:, 2 * u : 2 * u + 2, :])
+
+        w2_codes = [keep([P, 1024], U8, "w2_codes%d" % b) for b in range(2)]
+        w2_planes = [keep([P, 512], U8, "w2_plane%d" % b) for b in range(2)]
+        v2_plane = keep([P, R], U8, "v2_plane")
+        v2 = keep([P, R], U32, "v2")
+        for b in range(2):
+            nc.vector.tensor_copy(
+                out=w2_codes[b][:].rearrange("p (t m e) -> p t m e", t=PACK, e=2),
+                in_=w2_raw[:, 1024 * b : 1024 * (b + 1)].rearrange("p (m t e) -> p t m e", t=PACK, e=2),
+            )
+        load_gains(0)
+        for h in range(2):
+            nc.vector.tensor_copy(v2_plane[:, 256 * h : 256 * (h + 1)], tab2_plane[:].indirect(idx2[:, 16 * h : 16 * (h + 1)]))
+            nc.vector.tensor_copy(
+                out=w2_planes[h][:].rearrange("p (t m) -> p t m", t=PACK),
+                in_=w2_plane_raw[:, 512 * h : 512 * (h + 1)].rearrange("p (m t) -> p t m", t=PACK),
+            )
+            nc.vector.tensor_copy(v2[:, 256 * h : 256 * (h + 1)], tab2[:].indirect(idx2[:, 16 * h : 16 * (h + 1)]))
+
+        factors = {}
+        bent_slot = {(0, 0): "raw", (1, 0): "page01", (0, 1): "page11", (1, 1): "page02", (0, 2): "page03", (0, 3): "bias"}
+        factor_slot = {(0, 0): "tab0", (1, 0): "tab1", (0, 1): "gains1", (1, 1): "w4_plane", (0, 2): "w4_codes0", (0, 3): "w4_codes1",
+                       (1, 2): "factor12", (1, 3): "factor13"}
+
+        def make_factor(b, t, parts):
+            acc = psum.tile([P, W], F32, name="acc_b", tag="early", bufs=2)
+            if (b, t) in bent_slot:
+                bent = slot(bent_slot[b, t], [P, W], F32, "bent")
+            else:
+                bent = ring.tile([P, W], F32, name="bent", tag="bent", bufs=3, align_bytes=64)
+            factor = slot(factor_slot[b, t], [P, R], F32, "factor")
+            width = R // parts
+            for h in range(parts):
+                cols = slice(width * h, width * (h + 1))
+                nc.tensor.matmul_mx(
+                    out=acc[:, cols], lhsT=w2_codes[b][:, 256 * t : 256 * (t + 1)].bitcast(FP4X4),
+                    lhsT_scale=w2_planes[b][:, 128 * t : 128 * (t + 1)],
+                    rhs=v2[:, cols].bitcast(FP8X4), rhs_scale=v2_plane[:, cols], start=True, stop=True,
+                )
+                nc.scalar.activation(bent[:, cols], acc[:, cols], ACT.Tanh)
+                nc.scalar.activation(factor[:, cols], bent[:, cols], ACT.Exp)
+            factors[b, t] = factor
+
+        pages = {}
+
+        def new_page(b, t, zeroing):
+            page = slot("page%d%d" % (b, t), [P, S], F32, "page")
+            zeroing.memset(page[:], 0.0)
+            pages[b, t] = page
+
+        def place(b, t, parts):
+            width = R // parts
+            for h in range(parts):
+                cols = slice(width * h, width * (h + 1))
+                nc.vector.tensor_tensor(
+                    pages[b, t][:].indirect(places[:, width * h // 16 : width * (h + 1) // 16]),
+                    factors[b, t][:, cols], gains[t // 2][:, t % 2, cols], ALU.mult,
+                )
+
+        w1_codes, w1_planes = {}, {}
+        w1_raw = {}
+
+        def load_w1(a, b):
+            raw = raw_tile(F32, "w1_raw")
+            nc.sync.dma_start(
+                out=raw[:].rearrange("p (j c) -> p j c", j=PACK),
+                in_=w1[KP * a : KP * (a + 1), 512 * b : 512 * (b + 1)].rearrange("(p j) c -> p j c", j=PACK),
+            )
+            w1_raw[a, b] = raw
+
+        def quantize(woven, name):
+            codes = keep([P, 512], U32, name + "_codes")
+            plane = keep([P, 512], U8, name + "_plane")
+            nc.vector.quantize_mx(out=codes[:].bitcast(FP8X4), scales=plane[:], in_=woven[:])
+            return codes, plane
+
+        def quantize_w1(a, b):
+            woven = woven_tile("w1_woven")
+            nc.scalar.copy(
+                out=woven[:].rearrange("p (t m j) -> p m j t", t=PACK, j=PACK),
+                in_=w1_raw[a, b][:].rearrange("p (j m t) -> p m j t", j=PACK, t=PACK),
+            )
+            w1_codes[a, b], w1_planes[a, b] = quantize(woven, "w1_%d%d" % (a, b))
+
+        make_factor(0, 0, 2)
+        new_page(0, 0, nc.vector)
+        place(0, 0, 2)
+        make_factor(1, 0, 1)
+        new_page(1, 0, nc.vector)
+        place(1, 0, 1)
+        load_w1(0, 0)
+        load_w1(1, 0)
+        load_w1(0, 1)
+        tab_plane = slot("tab_plane", [P, T], U8, "tab_plane")
+        load_scale_rows(tab_plane, tab_scales, nc.gpsimd, on_sync)
+        tab = [slot("tab%d" % a, [P, T], U32, "tab%d" % a) for a in range(2)]
+        for a in range(2):
+            nc.sync.dma_start(out=tab[a][:].bitcast(I32), in_=tab_words[a].rearrange("p t i -> p (t i)").bitcast(I32))
+        make_factor(0, 1, 1)
+        make_factor(1, 1, 1)
+        for b in range(2):
+            new_page(b, 1, nc.gpsimd)
+            place(b, 1, 1)
+        load_gains(1)
+
+        quantize_w1(0, 0)
+        load_w1(1, 1)
+        quantize_w1(1, 0)
+        make_factor(0, 2, 1)
+        make_factor(0, 3, 1)
+        bias = slot("bias", [P, 2, PACK], F32, "bias")
+        nc.sync.dma_start(out=bias[:], in_=b1.rearrange("(b p t) -> p b t", b=2, t=PACK))
+        quantize_w1(0, 1)
+        make_factor(1, 2, 1)
+        make_factor(1, 3, 1)
+        quantize_w1(1, 1)
+
+        v_plane = keep([P, S], U8, "v_plane")
+        nc.vector.tensor_copy(v_plane[:], tab_plane[:].indirect(idx[:]))
+        v = [keep([P, S], U32, "v%d" % a) for a in range(2)]
+        for a in range(2):
+            nc.vector.tensor_copy(v[a][:], tab[a][:].indirect(idx[:]))
+
+        for t in (2, 3):
+            new_page(0, t, nc.gpsimd)
+            place(0, t, 1)
+
+        w3_raw = []
+        for b in range(2):
+            raw = raw_tile(F32, "w3_raw")
+            nc.sync.dma_start(
+                out=raw[:].rearrange("p (j c) -> p j c", j=PACK),
+                in_=w3[KP * b : KP * (b + 1), :].rearrange("(p j) c -> p j c", j=PACK),
+            )
+            w3_raw.append(raw)
+        w4_plane = slot("w4_plane", [P, N], U8, "w4_plane")
+        load_scale_rows(w4_plane, w4_scales, nc.gpsimd, on_sync)
+        w4_codes = [slot("w4_codes%d" % b, [P, N], U32, "w4_codes%d" % b) for b in range(2)]
+        for b in range(2):
+            nc.sync.dma_start(out=w4_codes[b][:].bitcast(I32), in_=w4_words[b].rearrange("p n i -> p (n i)").bitcast(I32))
+
+        feats = {}
+
+        def make_features(b, c, t):
+            acc = psum.tile([P, W], F32, name="acc_a", tag="early", bufs=2)
+            for a in range(2):
+                nc.tensor.matmul_mx(
+                    out=acc[:], lhsT=w1_codes[a, b][:, 128 * t : 128 * (t + 1)].bitcast(FP8X4),
+                    lhsT_scale=w1_planes[a, b][:, 128 * t : 128 * (t + 1)],
+                    rhs=v[a][:, W * c : W * (c + 1)].bitcast(FP8X4), rhs_scale=v_plane[4 * a : P, W * c : W * (c + 1)],
+                    start=(a == 0), stop=(a == 1),
+                )
+            feat = cols_tile("feat")
+            nc.scalar.activation(feat[:], acc[:], ACT.Identity, bias=bias[:, b, t : t + 1])
+            feats[b, c, t] = feat
+
+        flats = {}
+
+        def strengthen(b, c, t):
+            if (b, c) not in flats:
+                flats[b, c] = ring.tile([P, PACK, W], BF16, name="flat", tag="flat", bufs=3, align_bytes=64)
+            nc.vector.scalar_tensor_tensor(
+                out=flats[b, c][:, t, :], in0=pages[b, t][:, W * c : W * (c + 1)], scalar=1.0, in1=feats[b, c, t][:],
+                op0=ALU.add, op1=ALU.mult,
+            )
+
+        z_woven, z_codes, z_planes = {}, {}, {}
+
+        def weave_z(b, c, copy):
+            woven = woven_tile("z_woven")
+            copy(
+                out=woven[:].rearrange("p (g i t) -> p g t i", i=4, t=PACK),
+                in_=flats[b, c][:].rearrange("p t (g i) -> p g t i", i=4),
+            )
+            z_woven[b, c] = woven
+
+        def quantize_z(b, c):
+            z_codes[b, c], z_planes[b, c] = quantize(z_woven[b, c], "z_%d%d" % (b, c))
+
+        w3_codes, w3_planes = {}, {}
+
+        def quantize_w3(b):
+            woven = woven_tile("w3_woven")
+            nc.scalar.copy(
+                out=woven[:].rearrange("p (g i j) -> p g j i", i=4, j=PACK),
+                in_=w3_raw[b][:].rearrange("p (j g i) -> p g j i", i=4, j=PACK),
+            )
+            w3_codes[b], w3_planes[b] = quantize(woven, "w3_%d" % b)
+
+        def score(c, n):
+            rows = slice(128 * n, 128 * (n + 1))
+            y = psum.tile([P, W], F32, name="y", tag="late", bufs=6)
+            y4 = psum.tile([P, W], F32, name="y4", tag="late", bufs=6)
+            for b in range(2):
+                nc.tensor.matmul_mx(
+                    out=y[:], lhsT=w3_codes[b][:, rows].bitcast(FP8X4), lhsT_scale=w3_planes[b][:, rows],
+                    rhs=z_codes[b, c][:].bitcast(FP8X4), rhs_scale=z_planes[b, c][:], start=(b == 0), stop=(b == 1),
+                )
+                nc.tensor.matmul_mx(
+                    out=y4[:], lhsT=w4_codes[b][:, rows].bitcast(FP8X4), lhsT_scale=w4_plane[4 * b : P, rows],
+                    rhs=z_codes[b, c][:].bitcast(FP8X4), rhs_scale=z_planes[b, c][:], start=(b == 0), stop=(b == 1),
+                )
+            bent = ring.tile([P, W], F32, name="silu", tag="bent", bufs=3, align_bytes=64)
+            nc.scalar.activation(bent[:], y[:], ACT.Silu)
+            result = cols_tile("result")
+            nc.vector.tensor_tensor(result[:], y4[:], bent[:], ALU.add)
+            nc.sync.dma_start(out=out[rows, W * c : W * (c + 1)], in_=result[:])
+
+        for c in range(2):
+            for t in range(PACK):
+                make_features(0, c, t)
+        for c in range(2):
+            for t in range(PACK):
+                strengthen(0, c, t)
+        weave_z(0, 0, nc.scalar.copy)
+        for c in range(2):
+            for t in range(PACK):
+                make_features(1, c, t)
+        pages[1, 2] = pages[0, 3]
+        pages[1, 3] = pages[0, 2]
+        place(1, 2, 1)
+        place(1, 3, 1)
+        weave_z(0, 1, nc.scalar.copy)
+        quantize_z(0, 0)
+        quantize_w3(0)
+        quantize_z(0, 1)
+        quantize_w3(1)
+        for t in range(PACK):
+            strengthen(1, 0, t)
+        weave_z(1, 0, nc.scalar.copy)
+        for t in range(PACK):
+            strengthen(1, 1, t)
+        quantize_z(1, 0)
+        weave_z(1, 1, nc.vector.tensor_copy)
+        quantize_z(1, 1)
+        for n in range(4):
+            score(0, n)
+        for n in range(4):
+            score(1, n)

@@ -39,7 +39,7 @@ def tile_list_note_fitness_scores_kernel(
             return ring.tile([P, 2048], dtype, name=name, tag="raw", bufs=3, align_bytes=64)
 
         def woven_tile(name):
-            return ring.tile([P, 2048], BF16, name=name, tag="woven", bufs=4, align_bytes=64)
+            return ring.tile([P, 2048], BF16, name=name, tag="woven", bufs=6, align_bytes=64)
 
         def cols_tile(name):
             return ring.tile([P, W], F32, name=name, tag="cols", bufs=16, align_bytes=64)
@@ -62,15 +62,15 @@ def tile_list_note_fitness_scores_kernel(
 
         idx2 = held.tile([P, R // 16], U16, name="idx2")
         nc.sync.dma_start(idx2[:], offs2)
-        w2_raw = slot("gains0", [P, 2 * H], U8, "w2_raw")
-        nc.sync.dma_start(out=w2_raw[:].bitcast(I32), in_=w2_words[0].bitcast(I32))
         places = held.tile([P, R // 16], U16, name="places")
         nc.sync.dma_start(places[:], pos1)
         idx = held.tile([P, S // 16], U16, name="idx")
         nc.sync.dma_start(idx[:], offs)
+        w2_raw = slot("gains0", [P, 2 * H], U8, "w2_raw")
+        nc.sync.dma_start(out=w2_raw[:].bitcast(I32), in_=w2_words[0].bitcast(I32))
         tab2 = raw_tile(U32, "tab2")
         nc.sync.dma_start(out=tab2[:].bitcast(I32), in_=tab2_words[0].rearrange("p t i -> p (t i)").bitcast(I32))
-        tab2_plane = slot("tab_plane", [P, T3], U8, "tab2_plane")
+        tab2_plane = slot("raw", [P, T3], U8, "tab2_plane")
         load_scale_rows(tab2_plane, tab2_scales, nc.vector, on_sync)
         w2_plane_raw = slot("raw", [P, H], U8, "w2_plane_raw")
         load_scale_rows(w2_plane_raw, w2_scales, nc.vector, [nc.sync, nc.sync, nc.sync, nc.gpsimd])
@@ -78,10 +78,12 @@ def tile_list_note_fitness_scores_kernel(
         wgs_rows = wgs.rearrange("(q t) j -> q t j", t=PACK)
         gains = {}
 
-        def load_gains(u):
-            gains[u] = slot("gains%d" % u, [P, 2, R], F32, "gains%d" % u)
+        def load_gains(t0, count):
+            tile = slot("gains%d" % t0, [P, count, R], F32, "gains%d" % t0)
             for g in range(4):
-                nc.sync.dma_start(out=gains[u][32 * g : 32 * g + 32, :, :], in_=wgs_rows[:, 2 * u : 2 * u + 2, :])
+                nc.sync.dma_start(out=tile[32 * g : 32 * g + 32, :, :], in_=wgs_rows[:, t0 : t0 + count, :])
+            for i in range(count):
+                gains[t0 + i] = tile[:, i, :]
 
         w2_codes = [keep([P, 1024], U8, "w2_codes%d" % b) for b in range(2)]
         w2_planes = [keep([P, 512], U8, "w2_plane%d" % b) for b in range(2)]
@@ -89,25 +91,32 @@ def tile_list_note_fitness_scores_kernel(
         v2 = keep([P, R], U32, "v2")
         for b in range(2):
             nc.vector.tensor_copy(
-                out=w2_codes[b][:].rearrange("p (t m e) -> p t m e", t=PACK, e=2),
-                in_=w2_raw[:, 1024 * b : 1024 * (b + 1)].rearrange("p (m t e) -> p t m e", t=PACK, e=2),
+                out=w2_codes[b][:].bitcast(U16).rearrange("p (t m) -> p t m", t=PACK),
+                in_=w2_raw[:, 1024 * b : 1024 * (b + 1)].bitcast(U16).rearrange("p (m t) -> p t m", t=PACK),
             )
-        load_gains(0)
-        for h in range(2):
-            nc.vector.tensor_copy(v2_plane[:, 256 * h : 256 * (h + 1)], tab2_plane[:].indirect(idx2[:, 16 * h : 16 * (h + 1)]))
+        load_gains(0, 2)
+
+        def deal_w2_plane(b, t0, t1):
             nc.vector.tensor_copy(
-                out=w2_planes[h][:].rearrange("p (t m) -> p t m", t=PACK),
-                in_=w2_plane_raw[:, 512 * h : 512 * (h + 1)].rearrange("p (m t) -> p t m", t=PACK),
+                out=w2_planes[b][:].rearrange("p (t m) -> p t m", t=PACK)[:, t0:t1, :],
+                in_=w2_plane_raw[:, 512 * b : 512 * (b + 1)].rearrange("p (m t) -> p t m", t=PACK)[:, t0:t1, :],
             )
+
+        for h in range(2):
             nc.vector.tensor_copy(v2[:, 256 * h : 256 * (h + 1)], tab2[:].indirect(idx2[:, 16 * h : 16 * (h + 1)]))
+            nc.vector.tensor_copy(v2_plane[:, 256 * h : 256 * (h + 1)], tab2_plane[:].indirect(idx2[:, 16 * h : 16 * (h + 1)]))
+            if h == 0:
+                deal_w2_plane(0, 0, 1)
+        deal_w2_plane(0, 1, PACK)
+        deal_w2_plane(1, 0, PACK)
 
         factors = {}
-        bent_slot = {(0, 0): "raw", (1, 0): "page01", (0, 1): "page11", (1, 1): "page02", (0, 2): "page03", (0, 3): "bias"}
-        factor_slot = {(0, 0): "tab0", (1, 0): "tab1", (0, 1): "gains1", (1, 1): "w4_plane", (0, 2): "w4_codes0", (0, 3): "w4_codes1",
+        bent_slot = {(0, 3): "bias"}
+        factor_slot = {(0, 0): "tab0", (0, 1): "tab1", (1, 0): "gains2", (1, 1): "w4_plane", (0, 2): "w4_codes0", (0, 3): "w4_codes1",
                        (1, 2): "factor12", (1, 3): "factor13"}
 
         def make_factor(b, t, parts):
-            acc = psum.tile([P, W], F32, name="acc_b", tag="early", bufs=2)
+            acc = psum.tile([P, W], F32, name="acc_b", tag="bank", bufs=8)
             if (b, t) in bent_slot:
                 bent = slot(bent_slot[b, t], [P, W], F32, "bent")
             else:
@@ -138,7 +147,7 @@ def tile_list_note_fitness_scores_kernel(
                 cols = slice(width * h, width * (h + 1))
                 nc.vector.tensor_tensor(
                     pages[b, t][:].indirect(places[:, width * h // 16 : width * (h + 1) // 16]),
-                    factors[b, t][:, cols], gains[t // 2][:, t % 2, cols], ALU.mult,
+                    factors[b, t][:, cols], gains[t][:, cols], ALU.mult,
                 )
 
         w1_codes, w1_planes = {}, {}
@@ -153,7 +162,11 @@ def tile_list_note_fitness_scores_kernel(
             w1_raw[a, b] = raw
 
         def quantize(woven, name):
-            codes = keep([P, 512], U32, name + "_codes")
+            codes_slot = {"z_00": "factor13", "w1_01": "tab_plane", "w1_11": "tab0"}
+            if name in codes_slot:
+                codes = slot(codes_slot[name], [P, 512], U32, name + "_codes")
+            else:
+                codes = keep([P, 512], U32, name + "_codes")
             plane = keep([P, 512], U8, name + "_plane")
             nc.vector.quantize_mx(out=codes[:].bitcast(FP8X4), scales=plane[:], in_=woven[:])
             return codes, plane
@@ -169,23 +182,21 @@ def tile_list_note_fitness_scores_kernel(
         make_factor(0, 0, 2)
         new_page(0, 0, nc.vector)
         place(0, 0, 2)
-        make_factor(1, 0, 1)
-        new_page(1, 0, nc.vector)
-        place(1, 0, 1)
+        for b, t in ((0, 1), (1, 0)):
+            make_factor(b, t, 1)
+            new_page(b, t, nc.vector)
+            place(b, t, 1)
+        for t in (2, 3):
+            new_page(0, t, nc.vector)
         load_w1(0, 0)
         load_w1(1, 0)
         load_w1(0, 1)
         tab_plane = slot("tab_plane", [P, T], U8, "tab_plane")
-        load_scale_rows(tab_plane, tab_scales, nc.gpsimd, on_sync)
+        load_scale_rows(tab_plane, tab_scales, nc.vector, on_sync)
         tab = [slot("tab%d" % a, [P, T], U32, "tab%d" % a) for a in range(2)]
         for a in range(2):
             nc.sync.dma_start(out=tab[a][:].bitcast(I32), in_=tab_words[a].rearrange("p t i -> p (t i)").bitcast(I32))
-        make_factor(0, 1, 1)
-        make_factor(1, 1, 1)
-        for b in range(2):
-            new_page(b, 1, nc.gpsimd)
-            place(b, 1, 1)
-        load_gains(1)
+        load_gains(2, 2)
 
         quantize_w1(0, 0)
         load_w1(1, 1)
@@ -194,19 +205,18 @@ def tile_list_note_fitness_scores_kernel(
         make_factor(0, 3, 1)
         bias = slot("bias", [P, 2, PACK], F32, "bias")
         nc.sync.dma_start(out=bias[:], in_=b1.rearrange("(b p t) -> p b t", b=2, t=PACK))
-        quantize_w1(0, 1)
-        make_factor(1, 2, 1)
-        make_factor(1, 3, 1)
-        quantize_w1(1, 1)
 
         v_plane = keep([P, S], U8, "v_plane")
         nc.vector.tensor_copy(v_plane[:], tab_plane[:].indirect(idx[:]))
         v = [keep([P, S], U32, "v%d" % a) for a in range(2)]
         for a in range(2):
             nc.vector.tensor_copy(v[a][:], tab[a][:].indirect(idx[:]))
+        quantize_w1(0, 1)
+        for t in range(1, PACK):
+            make_factor(1, t, 1)
+        quantize_w1(1, 1)
 
         for t in (2, 3):
-            new_page(0, t, nc.gpsimd)
             place(0, t, 1)
 
         w3_raw = []
@@ -218,7 +228,7 @@ def tile_list_note_fitness_scores_kernel(
             )
             w3_raw.append(raw)
         w4_plane = slot("w4_plane", [P, N], U8, "w4_plane")
-        load_scale_rows(w4_plane, w4_scales, nc.gpsimd, on_sync)
+        load_scale_rows(w4_plane, w4_scales, nc.vector, on_sync)
         w4_codes = [slot("w4_codes%d" % b, [P, N], U32, "w4_codes%d" % b) for b in range(2)]
         for b in range(2):
             nc.sync.dma_start(out=w4_codes[b][:].bitcast(I32), in_=w4_words[b].rearrange("p n i -> p (n i)").bitcast(I32))
@@ -226,7 +236,7 @@ def tile_list_note_fitness_scores_kernel(
         feats = {}
 
         def make_features(b, c, t):
-            acc = psum.tile([P, W], F32, name="acc_a", tag="early", bufs=2)
+            acc = psum.tile([P, W], F32, name="acc_a", tag="bank", bufs=8)
             for a in range(2):
                 nc.tensor.matmul_mx(
                     out=acc[:], lhsT=w1_codes[a, b][:, 128 * t : 128 * (t + 1)].bitcast(FP8X4),
@@ -242,7 +252,7 @@ def tile_list_note_fitness_scores_kernel(
 
         def strengthen(b, c, t):
             if (b, c) not in flats:
-                flats[b, c] = ring.tile([P, PACK, W], BF16, name="flat", tag="flat", bufs=3, align_bytes=64)
+                flats[b, c] = ring.tile([P, PACK, W], BF16, name="flat", tag="flat", bufs=4, align_bytes=64)
             nc.vector.scalar_tensor_tensor(
                 out=flats[b, c][:, t, :], in0=pages[b, t][:, W * c : W * (c + 1)], scalar=1.0, in1=feats[b, c, t][:],
                 op0=ALU.add, op1=ALU.mult,
@@ -271,24 +281,28 @@ def tile_list_note_fitness_scores_kernel(
             )
             w3_codes[b], w3_planes[b] = quantize(woven, "w3_%d" % b)
 
-        def score(c, n):
+        banks = {}
+
+        def multiply(c, n, b, which, cols=slice(0, W)):
             rows = slice(128 * n, 128 * (n + 1))
-            y = psum.tile([P, W], F32, name="y", tag="late", bufs=6)
-            y4 = psum.tile([P, W], F32, name="y4", tag="late", bufs=6)
-            for b in range(2):
-                nc.tensor.matmul_mx(
-                    out=y[:], lhsT=w3_codes[b][:, rows].bitcast(FP8X4), lhsT_scale=w3_planes[b][:, rows],
-                    rhs=z_codes[b, c][:].bitcast(FP8X4), rhs_scale=z_planes[b, c][:], start=(b == 0), stop=(b == 1),
-                )
-                nc.tensor.matmul_mx(
-                    out=y4[:], lhsT=w4_codes[b][:, rows].bitcast(FP8X4), lhsT_scale=w4_plane[4 * b : P, rows],
-                    rhs=z_codes[b, c][:].bitcast(FP8X4), rhs_scale=z_planes[b, c][:], start=(b == 0), stop=(b == 1),
-                )
+            if b == 0:
+                banks[c, n, which] = psum.tile([P, W], F32, name="y", tag="bank", bufs=8)
+            if which == 3:
+                codes, plane = w3_codes[b][:, rows], w3_planes[b][:, rows]
+            else:
+                codes, plane = w4_codes[b][:, rows], w4_plane[4 * b : P, rows]
+            nc.tensor.matmul_mx(
+                out=banks[c, n, which][:, cols], lhsT=codes.bitcast(FP8X4), lhsT_scale=plane,
+                rhs=z_codes[b, c][:, cols].bitcast(FP8X4), rhs_scale=z_planes[b, c][:, cols],
+                start=(b == 0), stop=(b == 1 and cols.stop == W),
+            )
+
+        def finish(c, n):
             bent = ring.tile([P, W], F32, name="silu", tag="bent", bufs=3, align_bytes=64)
-            nc.scalar.activation(bent[:], y[:], ACT.Silu)
+            nc.scalar.activation(bent[:], banks[c, n, 3][:], ACT.Silu)
             result = cols_tile("result")
-            nc.vector.tensor_tensor(result[:], y4[:], bent[:], ALU.add)
-            nc.sync.dma_start(out=out[rows, W * c : W * (c + 1)], in_=result[:])
+            nc.vector.tensor_tensor(result[:], banks[c, n, 4][:], bent[:], ALU.add)
+            nc.sync.dma_start(out=out[128 * n : 128 * (n + 1), W * c : W * (c + 1)], in_=result[:])
 
         for c in range(2):
             for t in range(PACK):
@@ -296,28 +310,60 @@ def tile_list_note_fitness_scores_kernel(
         for c in range(2):
             for t in range(PACK):
                 strengthen(0, c, t)
-        weave_z(0, 0, nc.scalar.copy)
         for c in range(2):
             for t in range(PACK):
                 make_features(1, c, t)
-        pages[1, 2] = pages[0, 3]
-        pages[1, 3] = pages[0, 2]
-        place(1, 2, 1)
-        place(1, 3, 1)
+        weave_z(0, 0, nc.scalar.copy)
         weave_z(0, 1, nc.scalar.copy)
-        quantize_z(0, 0)
+        pages[1, 1] = pages[0, 3]
+        place(1, 1, 1)
+        pages[1, 2] = pages[0, 2]
+        place(1, 2, 1)
         quantize_w3(0)
-        quantize_z(0, 1)
         quantize_w3(1)
-        for t in range(PACK):
+        for t in range(3):
             strengthen(1, 0, t)
-        weave_z(1, 0, nc.scalar.copy)
-        for t in range(PACK):
-            strengthen(1, 1, t)
-        quantize_z(1, 0)
+        strengthen(1, 1, 0)
+        pages[1, 3] = pages[1, 0]
+        place(1, 3, 1)
+        strengthen(1, 0, 3)
+        half_woven = []
+        for h in range(2):
+            woven = woven_tile("z_woven")
+            nc.scalar.copy(
+                out=woven[:, 0:1024].rearrange("p (g i t) -> p g t i", i=4, t=PACK),
+                in_=flats[1, 0][:, :, 256 * h : 256 * (h + 1)].rearrange("p t (g i) -> p g t i", i=4),
+            )
+            half_woven.append(woven)
+        z_codes[1, 0] = keep([P, 512], U32, "z_10_codes")
+        z_planes[1, 0] = keep([P, 512], U8, "z_10_plane")
+
+        def second_pass_half(h):
+            cols = slice(256 * h, 256 * (h + 1))
+            nc.vector.quantize_mx(out=z_codes[1, 0][:, cols].bitcast(FP8X4), scales=z_planes[1, 0][:, cols], in_=half_woven[h][:, 0:1024])
+            for n in range(4):
+                for which in (3, 4):
+                    multiply(0, n, 1, which, cols)
+
+        quantize_z(0, 0)
+        for n in range(4):
+            for which in (3, 4):
+                multiply(0, n, 0, which)
+        strengthen(1, 1, 1)
+        second_pass_half(0)
+        strengthen(1, 1, 2)
+        strengthen(1, 1, 3)
+        second_pass_half(1)
+        quantize_z(0, 1)
         weave_z(1, 1, nc.vector.tensor_copy)
+        finish(0, 0)
         quantize_z(1, 1)
+        for n in range(1, 4):
+            finish(0, n)
         for n in range(4):
-            score(0, n)
+            multiply(1, n, 0, 3)
         for n in range(4):
-            score(1, n)
+            multiply(1, n, 0, 4)
+            multiply(1, n, 1, 3)
+            multiply(1, n, 1, 4)
+            finish(1, n)

@@ -39,7 +39,7 @@ def tile_list_note_fitness_scores_kernel(
             return ring.tile([P, 2048], dtype, name=name, tag="raw", bufs=3, align_bytes=64)
 
         def woven_tile(name):
-            return ring.tile([P, 2048], BF16, name=name, tag="woven", bufs=6, align_bytes=64)
+            return ring.tile([P, 2048], BF16, name=name, tag="woven", bufs=5, align_bytes=64)
 
         def cols_tile(name):
             return ring.tile([P, W], F32, name=name, tag="cols", bufs=16, align_bytes=64)
@@ -70,10 +70,10 @@ def tile_list_note_fitness_scores_kernel(
         nc.sync.dma_start(out=w2_raw[:].bitcast(I32), in_=w2_words[0].bitcast(I32))
         tab2 = raw_tile(U32, "tab2")
         nc.sync.dma_start(out=tab2[:].bitcast(I32), in_=tab2_words[0].rearrange("p t i -> p (t i)").bitcast(I32))
-        tab2_plane = slot("raw", [P, T3], U8, "tab2_plane")
+        tab2_plane = slot("tab_plane", [P, T3], U8, "tab2_plane")
         load_scale_rows(tab2_plane, tab2_scales, nc.vector, on_sync)
         w2_plane_raw = slot("raw", [P, H], U8, "w2_plane_raw")
-        load_scale_rows(w2_plane_raw, w2_scales, nc.vector, [nc.sync, nc.sync, nc.sync, nc.gpsimd])
+        load_scale_rows(w2_plane_raw, w2_scales, nc.gpsimd, [nc.sync, nc.sync, nc.sync, nc.gpsimd])
 
         wgs_rows = wgs.rearrange("(q t) j -> q t j", t=PACK)
         gains = {}
@@ -107,12 +107,12 @@ def tile_list_note_fitness_scores_kernel(
             nc.vector.tensor_copy(v2_plane[:, 256 * h : 256 * (h + 1)], tab2_plane[:].indirect(idx2[:, 16 * h : 16 * (h + 1)]))
             if h == 0:
                 deal_w2_plane(0, 0, 1)
-        deal_w2_plane(0, 1, PACK)
         deal_w2_plane(1, 0, PACK)
+        deal_w2_plane(0, 1, PACK)
 
         factors = {}
-        bent_slot = {(0, 3): "bias"}
-        factor_slot = {(0, 0): "tab0", (0, 1): "tab1", (1, 0): "gains2", (1, 1): "w4_plane", (0, 2): "w4_codes0", (0, 3): "w4_codes1",
+        bent_slot = {(0, 0): "raw", (1, 0): "page01", (0, 1): "page11", (1, 1): "page02", (0, 2): "page03"}
+        factor_slot = {(0, 0): "tab0", (1, 0): "tab1", (0, 1): "gains2", (1, 1): "w4_plane", (0, 2): "w4_codes0", (0, 3): "w4_codes1",
                        (1, 2): "factor12", (1, 3): "factor13"}
 
         def make_factor(b, t, parts):
@@ -162,9 +162,8 @@ def tile_list_note_fitness_scores_kernel(
             w1_raw[a, b] = raw
 
         def quantize(woven, name):
-            codes_slot = {"z_00": "factor13", "w1_01": "tab_plane", "w1_11": "tab0"}
-            if name in codes_slot:
-                codes = slot(codes_slot[name], [P, 512], U32, name + "_codes")
+            if name == "z_00":
+                codes = slot("z_00", [P, 512], U32, name + "_codes")
             else:
                 codes = keep([P, 512], U32, name + "_codes")
             plane = keep([P, 512], U8, name + "_plane")
@@ -182,53 +181,57 @@ def tile_list_note_fitness_scores_kernel(
         make_factor(0, 0, 2)
         new_page(0, 0, nc.vector)
         place(0, 0, 2)
-        for b, t in ((0, 1), (1, 0)):
-            make_factor(b, t, 1)
-            new_page(b, t, nc.vector)
-            place(b, t, 1)
-        for t in (2, 3):
-            new_page(0, t, nc.vector)
+        make_factor(1, 0, 1)
+        new_page(1, 0, nc.vector)
+        place(1, 0, 1)
         load_w1(0, 0)
         load_w1(1, 0)
         load_w1(0, 1)
         tab_plane = slot("tab_plane", [P, T], U8, "tab_plane")
-        load_scale_rows(tab_plane, tab_scales, nc.vector, on_sync)
+        load_scale_rows(tab_plane, tab_scales, nc.gpsimd, on_sync)
         tab = [slot("tab%d" % a, [P, T], U32, "tab%d" % a) for a in range(2)]
         for a in range(2):
             nc.sync.dma_start(out=tab[a][:].bitcast(I32), in_=tab_words[a].rearrange("p t i -> p (t i)").bitcast(I32))
+        make_factor(0, 1, 1)
+        make_factor(1, 1, 1)
+        for b in range(2):
+            new_page(b, 1, nc.gpsimd)
+            place(b, 1, 1)
         load_gains(2, 2)
 
+        w3_raw = {}
+
+        def load_w3(b):
+            raw = raw_tile(F32, "w3_raw")
+            nc.sync.dma_start(
+                out=raw[:].rearrange("p (j c) -> p j c", j=PACK),
+                in_=w3[KP * b : KP * (b + 1), :].rearrange("(p j) c -> p j c", j=PACK),
+            )
+            w3_raw[b] = raw
+
         quantize_w1(0, 0)
-        load_w1(1, 1)
+        load_w3(0)
         quantize_w1(1, 0)
+        load_w1(1, 1)
         make_factor(0, 2, 1)
         make_factor(0, 3, 1)
-        bias = slot("bias", [P, 2, PACK], F32, "bias")
-        nc.sync.dma_start(out=bias[:], in_=b1.rearrange("(b p t) -> p b t", b=2, t=PACK))
+        quantize_w1(0, 1)
+        load_w3(1)
+        make_factor(1, 2, 1)
+        make_factor(1, 3, 1)
 
         v_plane = keep([P, S], U8, "v_plane")
         nc.vector.tensor_copy(v_plane[:], tab_plane[:].indirect(idx[:]))
         v = [keep([P, S], U32, "v%d" % a) for a in range(2)]
         for a in range(2):
             nc.vector.tensor_copy(v[a][:], tab[a][:].indirect(idx[:]))
-        quantize_w1(0, 1)
-        for t in range(1, PACK):
-            make_factor(1, t, 1)
-        quantize_w1(1, 1)
 
         for t in (2, 3):
+            new_page(0, t, nc.gpsimd)
             place(0, t, 1)
 
-        w3_raw = []
-        for b in range(2):
-            raw = raw_tile(F32, "w3_raw")
-            nc.sync.dma_start(
-                out=raw[:].rearrange("p (j c) -> p j c", j=PACK),
-                in_=w3[KP * b : KP * (b + 1), :].rearrange("(p j) c -> p j c", j=PACK),
-            )
-            w3_raw.append(raw)
-        w4_plane = slot("w4_plane", [P, N], U8, "w4_plane")
-        load_scale_rows(w4_plane, w4_scales, nc.vector, on_sync)
+        w4_plane = slot("tab1", [P, N], U8, "w4_plane")
+        load_scale_rows(w4_plane, w4_scales, nc.gpsimd, on_sync)
         w4_codes = [slot("w4_codes%d" % b, [P, N], U32, "w4_codes%d" % b) for b in range(2)]
         for b in range(2):
             nc.sync.dma_start(out=w4_codes[b][:].bitcast(I32), in_=w4_words[b].rearrange("p n i -> p (n i)").bitcast(I32))
@@ -244,7 +247,10 @@ def tile_list_note_fitness_scores_kernel(
                     rhs=v[a][:, W * c : W * (c + 1)].bitcast(FP8X4), rhs_scale=v_plane[4 * a : P, W * c : W * (c + 1)],
                     start=(a == 0), stop=(a == 1),
                 )
-            feat = cols_tile("feat")
+            if (b, c, t) == (1, 1, 0):
+                feat = slot("z_00", [P, W], F32, "feat")
+            else:
+                feat = cols_tile("feat")
             nc.scalar.activation(feat[:], acc[:], ACT.Identity, bias=bias[:, b, t : t + 1])
             feats[b, c, t] = feat
 
@@ -261,7 +267,10 @@ def tile_list_note_fitness_scores_kernel(
         z_woven, z_codes, z_planes = {}, {}, {}
 
         def weave_z(b, c, copy):
-            woven = woven_tile("z_woven")
+            if (b, c) == (1, 1):
+                woven = slot("last_woven", [P, 2048], BF16, "z_woven")
+            else:
+                woven = woven_tile("z_woven")
             copy(
                 out=woven[:].rearrange("p (g i t) -> p g t i", i=4, t=PACK),
                 in_=flats[b, c][:].rearrange("p t (g i) -> p g t i", i=4),
@@ -304,32 +313,38 @@ def tile_list_note_fitness_scores_kernel(
             nc.vector.tensor_tensor(result[:], banks[c, n, 4][:], bent[:], ALU.add)
             nc.sync.dma_start(out=out[128 * n : 128 * (n + 1), W * c : W * (c + 1)], in_=result[:])
 
+        quantize_w3(0)
+        bias = slot("raw", [P, 2, PACK], F32, "bias")
+        nc.scalar.dma_start(out=bias[:], in_=b1.rearrange("(b p t) -> p b t", b=2, t=PACK))
+        quantize_w1(1, 1)
         for c in range(2):
             for t in range(PACK):
                 make_features(0, c, t)
         for c in range(2):
             for t in range(PACK):
                 strengthen(0, c, t)
-        for c in range(2):
-            for t in range(PACK):
-                make_features(1, c, t)
-        weave_z(0, 0, nc.scalar.copy)
-        weave_z(0, 1, nc.scalar.copy)
-        pages[1, 1] = pages[0, 3]
-        place(1, 1, 1)
-        pages[1, 2] = pages[0, 2]
+        pages[1, 2] = pages[0, 3]
         place(1, 2, 1)
-        quantize_w3(0)
         quantize_w3(1)
+        for t in range(PACK):
+            make_features(1, 0, t)
+        weave_z(0, 0, nc.scalar.copy)
+        for t in range(PACK):
+            make_features(1, 1, t)
+        weave_z(0, 1, nc.scalar.copy)
         for t in range(3):
             strengthen(1, 0, t)
         strengthen(1, 1, 0)
+        quantize_z(0, 0)
+        for n in range(4):
+            for which in (3, 4):
+                multiply(0, n, 0, which)
         pages[1, 3] = pages[1, 0]
         place(1, 3, 1)
         strengthen(1, 0, 3)
         half_woven = []
         for h in range(2):
-            woven = woven_tile("z_woven")
+            woven = slot("last_woven", [P, 2048], BF16, "z_woven") if h == 1 else woven_tile("z_woven")
             nc.scalar.copy(
                 out=woven[:, 0:1024].rearrange("p (g i t) -> p g t i", i=4, t=PACK),
                 in_=flats[1, 0][:, :, 256 * h : 256 * (h + 1)].rearrange("p t (g i) -> p g t i", i=4),
@@ -345,25 +360,23 @@ def tile_list_note_fitness_scores_kernel(
                 for which in (3, 4):
                     multiply(0, n, 1, which, cols)
 
-        quantize_z(0, 0)
-        for n in range(4):
-            for which in (3, 4):
-                multiply(0, n, 0, which)
         strengthen(1, 1, 1)
-        second_pass_half(0)
         strengthen(1, 1, 2)
+        second_pass_half(0)
         strengthen(1, 1, 3)
-        second_pass_half(1)
         quantize_z(0, 1)
+        second_pass_half(1)
         weave_z(1, 1, nc.vector.tensor_copy)
         finish(0, 0)
         quantize_z(1, 1)
         for n in range(1, 4):
             finish(0, n)
+        multiply(1, 0, 0, 3)
+        multiply(1, 0, 0, 4)
+        multiply(1, 1, 0, 3)
         for n in range(4):
-            multiply(1, n, 0, 3)
-        for n in range(4):
-            multiply(1, n, 0, 4)
-            multiply(1, n, 1, 3)
-            multiply(1, n, 1, 4)
+            for which in (3, 4):
+                if (1, n, which) not in banks:
+                    multiply(1, n, 0, which)
+                multiply(1, n, 1, which)
             finish(1, n)

from contextlib import ExitStack

import concourse.mybir as mybir

K, K2, T, T3, H, N, S, R = 1024, 512, 4096, 2048, 1024, 512, 1024, 512
FLOPS = 2 * (K * H * S + K2 * H * R + 2 * H * N * S)

F32 = mybir.dt.float32
BF16 = mybir.dt.bfloat16
I32 = mybir.dt.int32
U32 = mybir.dt.uint32
U16 = mybir.dt.uint16
U8 = mybir.dt.uint8
FP8X4 = mybir.dt.float8_e4m3fn_x4
FP4X4 = mybir.dt.float4_e2m1fn_x4
ACT = mybir.ActivationFunctionType
ALU = mybir.AluOpType

P = 128
PACK = 4
KP = 512
W = 512


def tile_list_note_fitness_scores_kernel(
    tc, tab_words, tab_scales, tab2_words, tab2_scales, offs, offs2, pos1,
    w1, b1, w2_words, w2_scales, wgs, w3, w4_words, w4_scales, out,
):
    nc = tc.nc
    with ExitStack() as ctx:
        held = ctx.enter_context(tc.tile_pool(name="held", bufs=1))
        ring = ctx.enter_context(tc.tile_pool(name="ring", bufs=1))
        psum = ctx.enter_context(tc.psum_pool(name="psum", bufs=1))

        def keep(shape, dtype, name):
            return held.tile(shape, dtype, name=name, align_bytes=64)

        def raw_tile(dtype, name):
            return ring.tile([P, 2048], dtype, name=name, tag="raw", bufs=3, align_bytes=64)

        def woven_tile(name):
            return ring.tile([P, 2048], BF16, name=name, tag="woven", bufs=5, align_bytes=64)

        def cols_tile(name):
            return ring.tile([P, W], F32, name=name, tag="cols", bufs=16, align_bytes=64)

        def slot(tag, shape, dtype, name):
            if tag == "raw":
                return ring.tile(shape, dtype, name=name, tag=tag, bufs=3, align_bytes=64)
            return ring.tile(shape, dtype, name=name, tag=tag, bufs=1, align_bytes=64)

        def load_scale_rows(plane, scales, zeroing, queues):
            passes = scales.shape[0]
            zeroing.memset(plane[:].bitcast(I32), 0)
            for q in range(4):
                queues[q].dma_start(
                    out=plane[32 * q : 32 * q + 4 * passes, :].bitcast(I32),
                    in_=scales[:, 4 * q : 4 * q + 4, :].bitcast(I32),
                )

        on_sync = [nc.sync] * 4

        idx2 = held.tile([P, R // 16], U16, name="idx2")
        nc.sync.dma_start(idx2[:], offs2)
        places = held.tile([P, R // 16], U16, name="places")
        nc.sync.dma_start(places[:], pos1)
        idx = held.tile([P, S // 16], U16, name="idx")
        nc.sync.dma_start(idx[:], offs)
        w2_raw = slot("gains0", [P, 2 * H], U8, "w2_raw")
        nc.sync.dma_start(out=w2_raw[:].bitcast(I32), in_=w2_words[0].bitcast(I32))
        tab2 = raw_tile(U32, "tab2")
        nc.sync.dma_start(out=tab2[:].bitcast(I32), in_=tab2_words[0].rearrange("p t i -> p (t i)").bitcast(I32))
        tab2_plane = slot("tab_plane", [P, T3], U8, "tab2_plane")
        load_scale_rows(tab2_plane, tab2_scales, nc.vector, on_sync)
        w2_plane_raw = slot("raw", [P, H], U8, "w2_plane_raw")
        load_scale_rows(w2_plane_raw, w2_scales, nc.gpsimd, [nc.sync, nc.sync, nc.sync, nc.gpsimd])

        wgs_rows = wgs.rearrange("(q t) j -> q t j", t=PACK)
        gains = {}

        def load_gains(t0, count):
            tile = slot("gains%d" % t0, [P, count, R], F32, "gains%d" % t0)
            for g in range(4):
                nc.sync.dma_start(out=tile[32 * g : 32 * g + 32, :, :], in_=wgs_rows[:, t0 : t0 + count, :])
            for i in range(count):
                gains[t0 + i] = tile[:, i, :]

        w2_codes = [keep([P, 1024], U8, "w2_codes%d" % b) for b in range(2)]
        w2_planes = [keep([P, 512], U8, "w2_plane%d" % b) for b in range(2)]
        v2_plane = keep([P, R], U8, "v2_plane")
        v2 = keep([P, R], U32, "v2")
        for b in range(2):
            nc.vector.tensor_copy(
                out=w2_codes[b][:].bitcast(U16).rearrange("p (t m) -> p t m", t=PACK),
                in_=w2_raw[:, 1024 * b : 1024 * (b + 1)].bitcast(U16).rearrange("p (m t) -> p t m", t=PACK),
            )
        load_gains(0, 2)

        def deal_w2_plane(b, t0, t1):
            nc.vector.tensor_copy(
                out=w2_planes[b][:].rearrange("p (t m) -> p t m", t=PACK)[:, t0:t1, :],
                in_=w2_plane_raw[:, 512 * b : 512 * (b + 1)].rearrange("p (m t) -> p t m", t=PACK)[:, t0:t1, :],
            )

        for h in range(2):
            nc.vector.tensor_copy(v2[:, 256 * h : 256 * (h + 1)], tab2[:].indirect(idx2[:, 16 * h : 16 * (h + 1)]))
            nc.vector.tensor_copy(v2_plane[:, 256 * h : 256 * (h + 1)], tab2_plane[:].indirect(idx2[:, 16 * h : 16 * (h + 1)]))
            if h == 0:
                deal_w2_plane(0, 0, 1)
        deal_w2_plane(1, 0, PACK)
        deal_w2_plane(0, 1, PACK)

        factors = {}
        bent_slot = {(0, 0): "raw", (1, 0): "page01", (0, 1): "page11", (1, 1): "page02", (0, 2): "page03"}
        factor_slot = {(0, 0): "tab0", (1, 0): "tab1", (0, 1): "gains2", (1, 1): "w4_plane", (0, 2): "w4_codes0", (0, 3): "w4_codes1",
                       (1, 2): "factor12", (1, 3): "factor13"}

        def make_factor(b, t, parts):
            acc = psum.tile([P, W], F32, name="acc_b", tag="bank", bufs=8)
            if (b, t) in bent_slot:
                bent = slot(bent_slot[b, t], [P, W], F32, "bent")
            else:
                bent = ring.tile([P, W], F32, name="bent", tag="bent", bufs=3, align_bytes=64)
            factor = slot(factor_slot[b, t], [P, R], F32, "factor")
            width = R // parts
            for h in range(parts):
                cols = slice(width * h, width * (h + 1))
                nc.tensor.matmul_mx(
                    out=acc[:, cols], lhsT=w2_codes[b][:, 256 * t : 256 * (t + 1)].bitcast(FP4X4),
                    lhsT_scale=w2_planes[b][:, 128 * t : 128 * (t + 1)],
                    rhs=v2[:, cols].bitcast(FP8X4), rhs_scale=v2_plane[:, cols], start=True, stop=True,
                )
                nc.scalar.activation(bent[:, cols], acc[:, cols], ACT.Tanh)
                nc.scalar.activation(factor[:, cols], bent[:, cols], ACT.Exp)
            factors[b, t] = factor

        pages = {}

        def new_page(b, t, zeroing):
            page = slot("page%d%d" % (b, t), [P, S], F32, "page")
            zeroing.memset(page[:], 0.0)
            pages[b, t] = page

        def place(b, t, parts):
            width = R // parts
            for h in range(parts):
                cols = slice(width * h, width * (h + 1))
                nc.vector.tensor_tensor(
                    pages[b, t][:].indirect(places[:, width * h // 16 : width * (h + 1) // 16]),
                    factors[b, t][:, cols], gains[t][:, cols], ALU.mult,
                )

        w1_codes, w1_planes = {}, {}
        w1_raw = {}

        def load_w1(a, b):
            raw = raw_tile(F32, "w1_raw")
            nc.sync.dma_start(
                out=raw[:].rearrange("p (j c) -> p j c", j=PACK),
                in_=w1[KP * a : KP * (a + 1), 512 * b : 512 * (b + 1)].rearrange("(p j) c -> p j c", j=PACK),
            )
            w1_raw[a, b] = raw

        def quantize(woven, name):
            if name == "z_00":
                codes = slot("z_00", [P, 512], U32, name + "_codes")
            else:
                codes = keep([P, 512], U32, name + "_codes")
            plane = keep([P, 512], U8, name + "_plane")
            nc.vector.quantize_mx(out=codes[:].bitcast(FP8X4), scales=plane[:], in_=woven[:])
            return codes, plane

        def quantize_w1(a, b):
            woven = woven_tile("w1_woven")
            nc.scalar.copy(
                out=woven[:].rearrange("p (t m j) -> p m j t", t=PACK, j=PACK),
                in_=w1_raw[a, b][:].rearrange("p (j m t) -> p m j t", j=PACK, t=PACK),
            )
            w1_codes[a, b], w1_planes[a, b] = quantize(woven, "w1_%d%d" % (a, b))

        make_factor(0, 0, 2)
        new_page(0, 0, nc.vector)
        place(0, 0, 2)
        make_factor(1, 0, 1)
        new_page(1, 0, nc.vector)
        place(1, 0, 1)
        load_w1(0, 0)
        load_w1(1, 0)
        load_w1(0, 1)
        tab_plane = slot("tab_plane", [P, T], U8, "tab_plane")
        load_scale_rows(tab_plane, tab_scales, nc.gpsimd, on_sync)
        tab = [slot("tab%d" % a, [P, T], U32, "tab%d" % a) for a in range(2)]
        for a in range(2):
            nc.sync.dma_start(out=tab[a][:].bitcast(I32), in_=tab_words[a].rearrange("p t i -> p (t i)").bitcast(I32))
        make_factor(0, 1, 1)
        make_factor(1, 1, 1)
        for b in range(2):
            new_page(b, 1, nc.gpsimd)
            place(b, 1, 1)
        load_gains(2, 2)

        w3_raw = {}

        def load_w3(b):
            raw = raw_tile(F32, "w3_raw")
            nc.sync.dma_start(
                out=raw[:].rearrange("p (j c) -> p j c", j=PACK),
                in_=w3[KP * b : KP * (b + 1), :].rearrange("(p j) c -> p j c", j=PACK),
            )
            w3_raw[b] = raw

        quantize_w1(0, 0)
        load_w3(0)
        quantize_w1(1, 0)
        load_w1(1, 1)
        make_factor(0, 2, 1)
        make_factor(0, 3, 1)
        quantize_w1(0, 1)
        load_w3(1)
        make_factor(1, 2, 1)
        make_factor(1, 3, 1)

        v_plane = keep([P, S], U8, "v_plane")
        nc.vector.tensor_copy(v_plane[:], tab_plane[:].indirect(idx[:]))
        v = [keep([P, S], U32, "v%d" % a) for a in range(2)]
        for a in range(2):
            nc.vector.tensor_copy(v[a][:], tab[a][:].indirect(idx[:]))

        for t in (2, 3):
            new_page(0, t, nc.gpsimd)
            place(0, t, 1)

        w4_plane = slot("tab1", [P, N], U8, "w4_plane")
        load_scale_rows(w4_plane, w4_scales, nc.gpsimd, on_sync)
        w4_codes = [slot("w4_codes%d" % b, [P, N], U32, "w4_codes%d" % b) for b in range(2)]
        for b in range(2):
            nc.sync.dma_start(out=w4_codes[b][:].bitcast(I32), in_=w4_words[b].rearrange("p n i -> p (n i)").bitcast(I32))

        feats = {}

        def make_features(b, c, t):
            acc = psum.tile([P, W], F32, name="acc_a", tag="bank", bufs=8)
            for a in range(2):
                nc.tensor.matmul_mx(
                    out=acc[:], lhsT=w1_codes[a, b][:, 128 * t : 128 * (t + 1)].bitcast(FP8X4),
                    lhsT_scale=w1_planes[a, b][:, 128 * t : 128 * (t + 1)],
                    rhs=v[a][:, W * c : W * (c + 1)].bitcast(FP8X4), rhs_scale=v_plane[4 * a : P, W * c : W * (c + 1)],
                    start=(a == 0), stop=(a == 1),
                )
            if (b, c, t) == (1, 1, 0):
                feat = slot("z_00", [P, W], F32, "feat")
            else:
                feat = cols_tile("feat")
            nc.scalar.activation(feat[:], acc[:], ACT.Identity, bias=bias[:, b, t : t + 1])
            feats[b, c, t] = feat

        flats = {}

        def strengthen(b, c, t):
            if (b, c) not in flats:
                flats[b, c] = ring.tile([P, PACK, W], BF16, name="flat", tag="flat", bufs=4, align_bytes=64)
            nc.vector.scalar_tensor_tensor(
                out=flats[b, c][:, t, :], in0=pages[b, t][:, W * c : W * (c + 1)], scalar=1.0, in1=feats[b, c, t][:],
                op0=ALU.add, op1=ALU.mult,
            )

        z_woven, z_codes, z_planes = {}, {}, {}

        def weave_z(b, c, copy):
            if (b, c) == (1, 1):
                woven = slot("last_woven", [P, 2048], BF16, "z_woven")
            else:
                woven = woven_tile("z_woven")
            copy(
                out=woven[:].rearrange("p (g i t) -> p g t i", i=4, t=PACK),
                in_=flats[b, c][:].rearrange("p t (g i) -> p g t i", i=4),
            )
            z_woven[b, c] = woven

        def quantize_z(b, c):
            z_codes[b, c], z_planes[b, c] = quantize(z_woven[b, c], "z_%d%d" % (b, c))

        w3_codes, w3_planes = {}, {}

        def quantize_w3(b):
            woven = woven_tile("w3_woven")
            nc.scalar.copy(
                out=woven[:].rearrange("p (g i j) -> p g j i", i=4, j=PACK),
                in_=w3_raw[b][:].rearrange("p (j g i) -> p g j i", i=4, j=PACK),
            )
            w3_codes[b], w3_planes[b] = quantize(woven, "w3_%d" % b)

        banks = {}

        def multiply(c, n, b, which, cols=slice(0, W)):
            rows = slice(128 * n, 128 * (n + 1))
            if b == 0:
                banks[c, n, which] = psum.tile([P, W], F32, name="y", tag="bank", bufs=8)
            if which == 3:
                codes, plane = w3_codes[b][:, rows], w3_planes[b][:, rows]
            else:
                codes, plane = w4_codes[b][:, rows], w4_plane[4 * b : P, rows]
            nc.tensor.matmul_mx(
                out=banks[c, n, which][:, cols], lhsT=codes.bitcast(FP8X4), lhsT_scale=plane,
                rhs=z_codes[b, c][:, cols].bitcast(FP8X4), rhs_scale=z_planes[b, c][:, cols],
                start=(b == 0), stop=(b == 1 and cols.stop == W),
            )

        def finish(c, n):
            bent = ring.tile([P, W], F32, name="silu", tag="bent", bufs=3, align_bytes=64)
            nc.scalar.activation(bent[:], banks[c, n, 3][:], ACT.Silu)
            result = cols_tile("result")
            nc.vector.tensor_tensor(result[:], banks[c, n, 4][:], bent[:], ALU.add)
            nc.sync.dma_start(out=out[128 * n : 128 * (n + 1), W * c : W * (c + 1)], in_=result[:])

        quantize_w3(0)
        bias = slot("raw", [P, 2, PACK], F32, "bias")
        nc.scalar.dma_start(out=bias[:], in_=b1.rearrange("(b p t) -> p b t", b=2, t=PACK))
        quantize_w1(1, 1)
        for c in range(2):
            for t in range(PACK):
                make_features(0, c, t)
        for c in range(2):
            for t in range(PACK):
                strengthen(0, c, t)
        pages[1, 2] = pages[0, 3]
        place(1, 2, 1)
        quantize_w3(1)
        for t in range(PACK):
            make_features(1, 0, t)
        weave_z(0, 0, nc.scalar.copy)
        for t in range(PACK):
            make_features(1, 1, t)
        weave_z(0, 1, nc.scalar.copy)
        for t in range(3):
            strengthen(1, 0, t)
        strengthen(1, 1, 0)
        quantize_z(0, 0)
        for n in range(4):
            for which in (3, 4):
                multiply(0, n, 0, which)
        pages[1, 3] = pages[1, 0]
        place(1, 3, 1)
        strengthen(1, 0, 3)
        half_woven = []
        for h in range(2):
            woven = slot("last_woven", [P, 2048], BF16, "z_woven") if h == 1 else woven_tile("z_woven")
            nc.scalar.copy(
                out=woven[:, 0:1024].rearrange("p (g i t) -> p g t i", i=4, t=PACK),
                in_=flats[1, 0][:, :, 256 * h : 256 * (h + 1)].rearrange("p t (g i) -> p g t i", i=4),
            )
            half_woven.append(woven)
        z_codes[1, 0] = keep([P, 512], U32, "z_10_codes")
        z_planes[1, 0] = keep([P, 512], U8, "z_10_plane")

        def second_pass_half(h):
            cols = slice(256 * h, 256 * (h + 1))
            nc.vector.quantize_mx(out=z_codes[1, 0][:, cols].bitcast(FP8X4), scales=z_planes[1, 0][:, cols], in_=half_woven[h][:, 0:1024])
            for n in range(4):
                for which in (3, 4):
                    multiply(0, n, 1, which, cols)

        strengthen(1, 1, 1)
        strengthen(1, 1, 2)
        second_pass_half(0)
        strengthen(1, 1, 3)
        quantize_z(0, 1)
        second_pass_half(1)
        weave_z(1, 1, nc.vector.tensor_copy)
        finish(0, 0)
        quantize_z(1, 1)
        for n in range(1, 4):
            finish(0, n)
        multiply(1, 0, 0, 3)
        multiply(1, 0, 0, 4)
        multiply(1, 1, 0, 3)
        for n in range(4):
            for which in (3, 4):
                if (1, n, which) not in banks:
                    multiply(1, n, 0, which)
                multiply(1, n, 1, which)
            finish(1, n)
